import numpy as np
import ml_dtypes


def mxq(x, axis, fmt="e4m3"):
    dtype, down = {"e4m3": (ml_dtypes.float8_e4m3fn, 7), "e5m2": (ml_dtypes.float8_e5m2, 14)}[fmt]
    v = np.moveaxis(np.asarray(x, np.float32).astype(ml_dtypes.bfloat16).astype(np.float64), axis, -1)
    blocks = v.reshape(v.shape[:-1] + (-1, 32))
    amax = np.abs(blocks).max(-1, keepdims=True)
    byte = np.maximum(np.where(amax > 0, np.frexp(amax)[1] - 1 + 127, 0) - down, 1)
    scale = np.exp2(byte - 127.0)
    codes = (blocks / scale).astype(np.float32).astype(dtype).astype(np.float64)
    return np.moveaxis((codes * scale).reshape(v.shape), -1, axis)


WIDE = False


def mx_kscale(k):
    if not WIDE:
        return np.ones(k)
    levels = np.array([10, -10, 5, -5, 0])
    if k % 512:
        return np.exp2(np.random.permutation(np.resize(levels, k // 32))).repeat(32)
    a = np.empty((k // 512, 16))
    for p in range(k // 512):
        a[p, :8] = np.random.permutation(np.resize(levels, 8))
        for g in range(8):
            far = levels[np.abs(levels - a[p, g]) >= 10]
            a[p, g + 8] = far[np.random.randint(len(far))]
    return np.exp2(a.ravel()).repeat(32)


def f64(x):
    return np.asarray(x).astype(np.float64)


def striped(idx):
    return np.tile(idx.reshape(-1, 16).T, (8, 1)).astype(np.uint16)


def unstriped(offs):
    return offs[:16].T.reshape(-1).astype(np.int64)


def silu(v):
    return v / (1.0 + np.exp(-np.maximum(v, -700.0)))


K, T, E, C, H, N = 512, 1536, 6, 128, 512, 512


def by_expert(wq, xq):
    return np.concatenate([wq[e].T @ xq[:, e * C:(e + 1) * C] for e in range(E)], axis=1)


def setup_inputs():
    n = np.random.standard_normal
    s = mx_kscale(K)[:, None]
    u = mx_kscale(H)
    return {
        "xT": (n((K, T)) * s).astype(np.float32),
        "w1": (n((E + 1, K, H)) / np.sqrt(K) / s[None] * u[None, None, :]).astype(np.float32),
        "w2": (n((E + 1, H, N)) / np.sqrt(H) / u[None, :, None]).astype(np.float32),
        "gate": np.tile(np.random.uniform(0.2, 1.0, E * C), (N, 1)).astype(np.float32),
        "offs": striped(np.random.permutation(T)[:E * C]),
    }


def reference(xT, w1, w2, gate, offs):
    idx = unstriped(offs)
    w1q, w2q = mxq(f64(w1), 1, "e4m3"), mxq(f64(w2), 1, "e4m3")
    xs = mxq(f64(xT), 0, "e4m3")
    hs = silu(w1q[E].T @ xs)
    ys = w2q[E].T @ mxq(hs, 0, "e4m3")
    xq = mxq(f64(xT)[:, idx], 0, "e4m3")
    h = silu(by_expert(w1q, xq))
    y = by_expert(w2q, mxq(h, 0, "e4m3"))
    out = ys
    out[:, idx] += f64(gate) * y
    return out

@@ -1,0 +1,215 @@
+from contextlib import ExitStack
+
+import concourse.mybir as mybir
+
+K, T, E, C, H, N = 512, 1536, 6, 128, 512, 512
+FLOPS = 2 * (E * C + T) * (K * H + H * N)
+BYTES = 4 * (K * T + (E + 1) * (K * H + H * N) + E * C + N * T) + 2 * 128 * (E * C // 16)
+
+P = 128
+PACK = 4
+PAIR = 2 * C
+GROUP = 512
+HALF = T // 2
+VECTOR_COLUMNS = {("w1", 0): 256,("w1", 1): 256,("w2", 0): 256,("w2", 1): 256,("w1", 2): 256,("w1", 4): 256,("w1", 5): 256,("w2", 6): 256}
+
+F32 = mybir.dt.float32
+BF16 = mybir.dt.bfloat16
+U32 = mybir.dt.uint32
+I32 = mybir.dt.int32
+U16 = mybir.dt.uint16
+U8 = mybir.dt.uint8
+FP8X4 = mybir.dt.float8_e4m3fn_x4
+MULT = mybir.AluOpType.mult
+ADD = mybir.AluOpType.add
+SILU = mybir.ActivationFunctionType.Silu
+
+
+def tile_moe_shr_mlp_silu_kernel(tc, xT, w1, w2, gate, offs, out):
+    nc = tc.nc
+    with ExitStack() as ctx:
+        index = ctx.enter_context(tc.tile_pool(name="index", bufs=1))
+        keep = ctx.enter_context(tc.tile_pool(name="keep", bufs=1))
+        stage = ctx.enter_context(tc.tile_pool(name="stage", bufs=1))
+        psum = ctx.enter_context(tc.psum_pool(name="psum", bufs=1))
+
+        offsets = index.tile([P, E * C // 16], U16, name="offsets")
+        xp = keep.tile([P, 2 * T * 2], BF16, name="xp", align_bytes=64)
+        xg = keep.tile([P, E * C * PACK], BF16, name="xg", align_bytes=64)
+        xs_codes = keep.tile([P, T], U32, name="xs_codes", align_bytes=64)
+        xs_scales = keep.tile([P, T], U8, name="xs_scales", align_bytes=64)
+        slot_codes = keep.tile([P, E * C], U32, name="slot_codes", align_bytes=64)
+        slot_scales = keep.tile([P, E * C], U8, name="slot_scales", align_bytes=64)
+        h_codes = keep.tile([P, E * C], U32, name="h_codes", align_bytes=64)
+        h_scales = keep.tile([P, E * C], U8, name="h_scales", align_bytes=64)
+        hs_codes = keep.tile([P, T], U32, name="hs_codes", align_bytes=64)
+        hs_scales = keep.tile([P, T], U8, name="hs_scales", align_bytes=64)
+        gates = keep.tile([P, E * C], F32, name="gates")
+        acc = [keep.tile([P, T], F32, name=f"acc{q}") for q in range(4)]
+        warm = keep.tile([P, 1], F32, name="warm")
+
+        def quantize(rounded, codes, scales):
+            nc.vector.quantize_mx(out=codes.bitcast(FP8X4), scales=scales, in_=rounded)
+
+        w_codes = {}
+
+        def weight(layer, e):
+            matrix = (w1 if layer == "w1" else w2)[e]
+            raw = stage.tile([P, PACK, 512], F32, name="raw", bufs=8)
+            nc.sync.dma_start(out=raw[:], in_=matrix.rearrange("(p j) w -> p j w", j=PACK))
+            rounded = stage.tile([P, 512 * PACK], BF16, name="rounded", bufs=4, align_bytes=64)
+            if layer == "w1":
+                dst = rounded[:].rearrange("p (t m j) -> p m j t", t=PACK, j=PACK)
+                src = raw[:].rearrange("p j (m t) -> p m j t", t=PACK)
+            else:
+                dst = rounded[:].rearrange("p (c i j) -> p c j i", i=4, j=PACK)
+                src = raw[:].rearrange("p j (c i) -> p c j i", i=4)
+            cut = 128 - VECTOR_COLUMNS.get((layer, e), 0) // 4
+            if cut > 0:
+                nc.scalar.copy(dst[:, :cut], src[:, :cut])
+            if cut < 128:
+                nc.vector.tensor_copy(dst[:, cut:], src[:, cut:])
+            codes = keep.tile([P, 512], U32, name=f"codes_{layer}_{e}", align_bytes=64)
+            scales = keep.tile([P, 512], U8, name=f"scales_{layer}_{e}", align_bytes=64)
+            quantize(rounded[:], codes[:], scales[:])
+            w_codes[layer, e] = (codes, scales)
+
+        def multiply(bank, w, w_cols, act_codes, act_scales):
+            nc.tensor.matmul_mx(
+                out=bank,
+                lhsT=w[0][:, w_cols].bitcast(FP8X4),
+                lhsT_scale=w[1][:, w_cols],
+                rhs=act_codes.bitcast(FP8X4),
+                rhs_scale=act_scales,
+                start=True,
+                stop=True,
+            )
+
+        def first_layer(e, act_codes, act_scales, hidden):
+            bank = psum.tile([P, PACK, C], F32, name="bank_a", bufs=3)
+            for t in range(PACK):
+                multiply(bank[:, t, :], w_codes["w1", e], slice(128 * t, 128 * t + 128), act_codes, act_scales)
+            nc.scalar.activation(
+                hidden.rearrange("p (n t) -> p n t", t=PACK), bank[:].rearrange("p t n -> p n t"), SILU
+            )
+
+        nc.vector.memset(warm[:], 0.0)
+        nc.scalar.activation(warm[:], warm[:], SILU)
+        nc.vector.memset(acc[0][:], 0.0)
+        nc.vector.memset(acc[1][:], 0.0)
+        nc.gpsimd.memset(acc[2][:], 0.0)
+        nc.gpsimd.memset(acc[3][:], 0.0)
+
+        xp_words = xp[:].bitcast(I32).rearrange("p (u t) -> p u t", u=2)
+        xp_pairs = xp[:].rearrange("p (u t e) -> p u t e", u=2, e=2)
+        window = xp[:].bitcast(U32)
+        slot_words = xg[:].bitcast(U32).rearrange("p (s u) -> p s u", u=2)
+        x_rows = xT.rearrange("(p u e) t -> p u e t", u=2, e=2)
+
+        def tokens(u, half, copy):
+            cols = slice(half * HALF, (half + 1) * HALF)
+            raw = stage.tile([P, 2, HALF], F32, name="raw", bufs=8)
+            nc.sync.dma_start(out=raw[:], in_=x_rows[:, u, :, cols])
+            copy(
+                xp_pairs[:, u, cols, :].rearrange("p (c i) e -> p c e i", i=4),
+                raw[:].rearrange("p e (c i) -> p c e i", i=4),
+            )
+
+        def gather(u):
+            nc.vector.tensor_copy(slot_words[:, :, u], window[:, u * T : (u + 1) * T].indirect(offsets[:]))
+
+        def quantize_slots(pair):
+            slots = slice(pair * PAIR, (pair + 1) * PAIR)
+            quantize(xg[:, pair * PAIR * PACK : (pair + 1) * PAIR * PACK], slot_codes[:, slots], slot_scales[:, slots])
+
+        def shared_tokens(g):
+            cols = slice(g * GROUP, (g + 1) * GROUP)
+            xi = stage.tile([P, GROUP * PACK], BF16, name="xi", bufs=2, align_bytes=64)
+            nc.vector.tensor_copy(
+                xi[:].bitcast(I32).rearrange("p (t u) -> p t u", u=2),
+                xp_words[:, :, cols].rearrange("p u t -> p t u"),
+            )
+            quantize(xi[:], xs_codes[:, cols], xs_scales[:, cols])
+
+        def hidden_slots(e):
+            slots = slice(e * C, (e + 1) * C)
+            hidden = stage.tile([P, C * PACK], BF16, name="hidden", bufs=3, align_bytes=64)
+            first_layer(e, slot_codes[:, slots], slot_scales[:, slots], hidden[:])
+            quantize(hidden[:], h_codes[:, slots], h_scales[:, slots])
+
+        results = {}
+
+        def results_of(e):
+            pair, half = e // 2, e % 2
+            if half == 0:
+                results[pair] = stage.tile([P, 4, PAIR], F32, name="results", bufs=2)
+            slots = slice(e * C, (e + 1) * C)
+            bank = psum.tile([P, 4, C], F32, name="bank_y", bufs=2)
+            for q in range(4):
+                multiply(bank[:, q, :], w_codes["w2", e], slice(128 * q, 128 * q + 128), h_codes[:, slots], h_scales[:, slots])
+            nc.scalar.copy(results[pair][:, :, half * C : (half + 1) * C], bank[:])
+
+        def scatter(pair, q):
+            listed = offsets[:, pair * PAIR // 16 : (pair + 1) * PAIR // 16]
+            weights = gates[:, pair * PAIR : (pair + 1) * PAIR]
+            nc.vector.tensor_tensor(acc[q][:].indirect(listed), results[pair][:, q, :], weights, MULT)
+
+        def shared_hidden(g):
+            hs = stage.tile([P, GROUP * PACK], BF16, name="hs", bufs=2, align_bytes=64)
+            for b in range(GROUP // C):
+                cols = slice(g * GROUP + b * C, g * GROUP + (b + 1) * C)
+                first_layer(E, xs_codes[:, cols], xs_scales[:, cols], hs[:, b * 512 : (b + 1) * 512])
+            cols = slice(g * GROUP, (g + 1) * GROUP)
+            quantize(hs[:], hs_codes[:, cols], hs_scales[:, cols])
+
+        def finish(q, g):
+            cols = slice(g * GROUP, (g + 1) * GROUP)
+            rows = slice(128 * q, 128 * q + 128)
+            bank = psum.tile([P, GROUP], F32, name="bank_s", bufs=3)
+            multiply(bank[:], w_codes["w2", E], rows, hs_codes[:, cols], hs_scales[:, cols])
+            if False:
+                ys = stage.tile([P, GROUP], F32, name="ys", bufs=3)
+                nc.scalar.copy(ys[:], bank[:])
+                nc.gpsimd.tensor_tensor(acc[q][:, cols], ys[:], acc[q][:, cols], ADD)
+            else:
+                nc.vector.tensor_tensor(acc[q][:, cols], bank[:], acc[q][:, cols], ADD)
+            nc.sync.dma_start(out=out[rows, cols], in_=acc[q][:, cols])
+
+        def load_offsets():
+            nc.sync.dma_start(offsets[:], offs)
+
+        tokens(0, 0, nc.scalar.copy)
+        load_offsets()
+        tokens(0, 1, nc.vector.tensor_copy)
+        tokens(1, 0, nc.vector.tensor_copy)
+        tokens(1, 1, nc.scalar.copy)
+        gather(0)
+        gather(1)
+        for pair in range(3):
+            quantize_slots(pair)
+        for pair in range(3):
+            a, b = 2 * pair, 2 * pair + 1
+            weight("w1", a)
+            weight("w1", b)
+            hidden_slots(a)
+            hidden_slots(b)
+            weight("w2", a)
+            weight("w2", b)
+            results_of(a)
+            results_of(b)
+            if pair == 0:
+                nc.sync.dma_start(out=gates[:], in_=gate[0:P, :])
+            if pair == 1:
+                weight("w1", E)
+                for g in range(3):
+                    shared_tokens(g)
+                    shared_hidden(g)
+                weight("w2", E)
+            if pair < 2:
+                for q in range(4):
+                    scatter(pair, q)
+        for q in (3, 0, 1, 2):
+            scatter(2, q)
+        for q in (3, 0, 1, 2):
+            for g in range(T // GROUP):
+                finish(q, g)

@@ -11,7 +11,7 @@ PACK = 4
 PAIR = 2 * C
 GROUP = 512
 HALF = T // 2
-VECTOR_COLUMNS = {("w1", 0): 256,("w1", 1): 256,("w2", 0): 256,("w2", 1): 256,("w1", 2): 256,("w1", 4): 256,("w1", 5): 256,("w2", 6): 256}
+VECTOR_COLUMNS = {("w1", 0): 128,("w1", 1): 0,("w2", 0): 0,("w2", 1): 256,("w1", 2): 128,("w1", 3): 0,("w2", 2): 0,("w2", 3): 256,("w1", 4): 128,("w1", 5): 0,("w2", 4): 0,("w2", 5): 256,("w1", 6): 0,("w2", 6): 512}
 
 F32 = mybir.dt.float32
 BF16 = mybir.dt.bfloat16
@@ -52,10 +52,11 @@ def tile_moe_shr_mlp_silu_kernel(tc, xT, w1, w2, gate, offs, out):
             nc.vector.quantize_mx(out=codes.bitcast(FP8X4), scales=scales, in_=rounded)
 
         w_codes = {}
+        raws = {}
 
         def weight(layer, e):
             matrix = (w1 if layer == "w1" else w2)[e]
-            raw = stage.tile([P, PACK, 512], F32, name="raw", bufs=8)
+            raw = stage.tile([P, PACK, 512], F32, name="raw", bufs=8, align_bytes=64)
             nc.sync.dma_start(out=raw[:], in_=matrix.rearrange("(p j) w -> p j w", j=PACK))
             rounded = stage.tile([P, 512 * PACK], BF16, name="rounded", bufs=4, align_bytes=64)
             if layer == "w1":
@@ -73,6 +74,7 @@ def tile_moe_shr_mlp_silu_kernel(tc, xT, w1, w2, gate, offs, out):
             scales = keep.tile([P, 512], U8, name=f"scales_{layer}_{e}", align_bytes=64)
             quantize(rounded[:], codes[:], scales[:])
             w_codes[layer, e] = (codes, scales)
+            raws[layer, e] = raw
 
         def multiply(bank, w, w_cols, act_codes, act_scales):
             nc.tensor.matmul_mx(
@@ -108,7 +110,7 @@ def tile_moe_shr_mlp_silu_kernel(tc, xT, w1, w2, gate, offs, out):
 
         def tokens(u, half, copy):
             cols = slice(half * HALF, (half + 1) * HALF)
-            raw = stage.tile([P, 2, HALF], F32, name="raw", bufs=8)
+            raw = stage.tile([P, 2, HALF], F32, name="raw", bufs=8, align_bytes=64)
             nc.sync.dma_start(out=raw[:], in_=x_rows[:, u, :, cols])
             copy(
                 xp_pairs[:, u, cols, :].rearrange("p (c i) e -> p c e i", i=4),
@@ -133,9 +135,13 @@ def tile_moe_shr_mlp_silu_kernel(tc, xT, w1, w2, gate, offs, out):
 
         def hidden_slots(e):
             slots = slice(e * C, (e + 1) * C)
-            hidden = stage.tile([P, C * PACK], BF16, name="hidden", bufs=3, align_bytes=64)
-            first_layer(e, slot_codes[:, slots], slot_scales[:, slots], hidden[:])
-            quantize(hidden[:], h_codes[:, slots], h_scales[:, slots])
+            if e // 2 in (1,):
+                hidden = raws["w2", e][:].rearrange("p j w -> p (j w)").bitcast(BF16)[:, : C * PACK]
+            else:
+                fresh = stage.tile([P, C * PACK], BF16, name="hidden", bufs=3, align_bytes=64)
+                hidden = fresh[:]
+            first_layer(e, slot_codes[:, slots], slot_scales[:, slots], hidden)
+            quantize(hidden, h_codes[:, slots], h_scales[:, slots])
 
         results = {}
 
@@ -167,48 +173,63 @@ def tile_moe_shr_mlp_silu_kernel(tc, xT, w1, w2, gate, offs, out):
             rows = slice(128 * q, 128 * q + 128)
             bank = psum.tile([P, GROUP], F32, name="bank_s", bufs=3)
             multiply(bank[:], w_codes["w2", E], rows, hs_codes[:, cols], hs_scales[:, cols])
-            if False:
+            if q == 3:
                 ys = stage.tile([P, GROUP], F32, name="ys", bufs=3)
                 nc.scalar.copy(ys[:], bank[:])
                 nc.gpsimd.tensor_tensor(acc[q][:, cols], ys[:], acc[q][:, cols], ADD)
             else:
                 nc.vector.tensor_tensor(acc[q][:, cols], bank[:], acc[q][:, cols], ADD)
-            nc.sync.dma_start(out=out[rows, cols], in_=acc[q][:, cols])
+            queue = nc.scalar if q == 3 else nc.sync
+            queue.dma_start(out=out[rows, cols], in_=acc[q][:, cols])
 
-        def load_offsets():
-            nc.sync.dma_start(offsets[:], offs)
-
-        tokens(0, 0, nc.scalar.copy)
-        load_offsets()
+        tokens(0, 0, nc.vector.tensor_copy)
+        nc.sync.dma_start(offsets[:], offs)
         tokens(0, 1, nc.vector.tensor_copy)
-        tokens(1, 0, nc.vector.tensor_copy)
+        tokens(1, 0, nc.scalar.copy)
         tokens(1, 1, nc.scalar.copy)
         gather(0)
         gather(1)
-        for pair in range(3):
-            quantize_slots(pair)
-        for pair in range(3):
-            a, b = 2 * pair, 2 * pair + 1
-            weight("w1", a)
-            weight("w1", b)
-            hidden_slots(a)
-            hidden_slots(b)
-            weight("w2", a)
-            weight("w2", b)
-            results_of(a)
-            results_of(b)
-            if pair == 0:
-                nc.sync.dma_start(out=gates[:], in_=gate[0:P, :])
-            if pair == 1:
-                weight("w1", E)
-                for g in range(3):
-                    shared_tokens(g)
-                    shared_hidden(g)
-                weight("w2", E)
-            if pair < 2:
-                for q in range(4):
-                    scatter(pair, q)
-        for q in (3, 0, 1, 2):
+        quantize_slots(0)
+        quantize_slots(1)
+        quantize_slots(2)
+        weight("w1", 0)
+        weight("w1", 1)
+        hidden_slots(0)
+        hidden_slots(1)
+        weight("w2", 0)
+        weight("w2", 1)
+        results_of(0)
+        results_of(1)
+        nc.sync.dma_start(out=gates[:], in_=gate[0:P, :])
+        shared_tokens(0)
+        shared_tokens(1)
+        shared_tokens(2)
+        weight("w1", E)
+        weight("w1", 2)
+        weight("w1", 3)
+        weight("w2", 2)
+        weight("w2", 3)
+        hidden_slots(2)
+        hidden_slots(3)
+        results_of(2)
+        results_of(3)
+        for q in range(4):
+            scatter(0, q)
+        weight("w1", 4)
+        weight("w1", 5)
+        weight("w2", 4)
+        weight("w2", 5)
+        hidden_slots(4)
+        hidden_slots(5)
+        results_of(4)
+        results_of(5)
+        weight("w2", E)
+        for q in range(4):
+            scatter(1, q)
+        shared_hidden(0)
+        shared_hidden(1)
+        shared_hidden(2)
+        for q in range(4):
             scatter(2, q)
         for q in (3, 0, 1, 2):
             for g in range(T // GROUP):

@@ -11,7 +11,7 @@ PACK = 4
 PAIR = 2 * C
 GROUP = 512
 HALF = T // 2
-VECTOR_COLUMNS = {("w1", 0): 128,("w1", 1): 0,("w2", 0): 0,("w2", 1): 256,("w1", 2): 128,("w1", 3): 0,("w2", 2): 0,("w2", 3): 256,("w1", 4): 128,("w1", 5): 0,("w2", 4): 0,("w2", 5): 256,("w1", 6): 0,("w2", 6): 512}
+VECTOR_COLUMNS = {("w1", 0): 192,("w1", 1): 0,("w2", 0): 0,("w2", 1): 256,("w1", 2): 192,("w1", 3): 0,("w2", 2): 0,("w2", 3): 256,("w1", 4): 192,("w1", 5): 0,("w2", 4): 0,("w2", 5): 256,("w1", 6): 0,("w2", 6): 512}
 
 F32 = mybir.dt.float32
 BF16 = mybir.dt.bfloat16
@@ -201,18 +201,18 @@ def tile_moe_shr_mlp_silu_kernel(tc, xT, w1, w2, gate, offs, out):
         results_of(0)
         results_of(1)
         nc.sync.dma_start(out=gates[:], in_=gate[0:P, :])
-        shared_tokens(0)
-        shared_tokens(1)
-        shared_tokens(2)
-        weight("w1", E)
         weight("w1", 2)
         weight("w1", 3)
+        weight("w1", E)
         weight("w2", 2)
         weight("w2", 3)
         hidden_slots(2)
         hidden_slots(3)
         results_of(2)
         results_of(3)
+        shared_tokens(0)
+        shared_tokens(1)
+        shared_tokens(2)
         for q in range(4):
             scatter(0, q)
         weight("w1", 4)
@@ -223,10 +223,10 @@ def tile_moe_shr_mlp_silu_kernel(tc, xT, w1, w2, gate, offs, out):
         hidden_slots(5)
         results_of(4)
         results_of(5)
-        weight("w2", E)
+        shared_hidden(0)
         for q in range(4):
             scatter(1, q)
-        shared_hidden(0)
+        weight("w2", E)
         shared_hidden(1)
         shared_hidden(2)
         for q in range(4):

@@ -68,8 +68,13 @@ def tile_moe_shr_mlp_silu_kernel(tc, xT, w1, w2, gate, offs, out):
             cut = 128 - VECTOR_COLUMNS.get((layer, e), 0) // 4
             if cut > 0:
                 nc.scalar.copy(dst[:, :cut], src[:, :cut])
-            if cut < 128:
+            if cut < 128 and layer == "w1":
                 nc.vector.tensor_copy(dst[:, cut:], src[:, cut:])
+            elif cut < 128:
+                nc.vector.tensor_copy(
+                    rounded[:, 16 * cut :].rearrange("p (c j) -> p c j", j=PACK),
+                    raw[:, :, 4 * cut :].rearrange("p j c -> p c j"),
+                )
             codes = keep.tile([P, 512], U32, name=f"codes_{layer}_{e}", align_bytes=64)
             scales = keep.tile([P, 512], U8, name=f"scales_{layer}_{e}", align_bytes=64)
             quantize(rounded[:], codes[:], scales[:])
@@ -108,14 +113,17 @@ def tile_moe_shr_mlp_silu_kernel(tc, xT, w1, w2, gate, offs, out):
         slot_words = xg[:].bitcast(U32).rearrange("p (s u) -> p s u", u=2)
         x_rows = xT.rearrange("(p u e) t -> p u e t", u=2, e=2)
 
-        def tokens(u, half, copy):
+        def tokens(u, half, vector):
             cols = slice(half * HALF, (half + 1) * HALF)
             raw = stage.tile([P, 2, HALF], F32, name="raw", bufs=8, align_bytes=64)
             nc.sync.dma_start(out=raw[:], in_=x_rows[:, u, :, cols])
-            copy(
-                xp_pairs[:, u, cols, :].rearrange("p (c i) e -> p c e i", i=4),
-                raw[:].rearrange("p e (c i) -> p c e i", i=4),
-            )
+            if vector:
+                nc.vector.tensor_copy(xp_pairs[:, u, cols, :], raw[:].rearrange("p e t -> p t e"))
+            else:
+                nc.scalar.copy(
+                    xp_pairs[:, u, cols, :].rearrange("p (c i) e -> p c e i", i=4),
+                    raw[:].rearrange("p e (c i) -> p c e i", i=4),
+                )
 
         def gather(u):
             nc.vector.tensor_copy(slot_words[:, :, u], window[:, u * T : (u + 1) * T].indirect(offsets[:]))
@@ -135,7 +143,7 @@ def tile_moe_shr_mlp_silu_kernel(tc, xT, w1, w2, gate, offs, out):
 
         def hidden_slots(e):
             slots = slice(e * C, (e + 1) * C)
-            if e // 2 in (1,):
+            if e // 2 in (0, 1,):
                 hidden = raws["w2", e][:].rearrange("p j w -> p (j w)").bitcast(BF16)[:, : C * PACK]
             else:
                 fresh = stage.tile([P, C * PACK], BF16, name="hidden", bufs=3, align_bytes=64)
@@ -182,11 +190,11 @@ def tile_moe_shr_mlp_silu_kernel(tc, xT, w1, w2, gate, offs, out):
             queue = nc.scalar if q == 3 else nc.sync
             queue.dma_start(out=out[rows, cols], in_=acc[q][:, cols])
 
-        tokens(0, 0, nc.vector.tensor_copy)
+        tokens(0, 0, True)
         nc.sync.dma_start(offsets[:], offs)
-        tokens(0, 1, nc.vector.tensor_copy)
-        tokens(1, 0, nc.scalar.copy)
-        tokens(1, 1, nc.scalar.copy)
+        tokens(0, 1, True)
+        tokens(1, 0, False)
+        tokens(1, 1, False)
         gather(0)
         gather(1)
         quantize_slots(0)
@@ -194,13 +202,16 @@ def tile_moe_shr_mlp_silu_kernel(tc, xT, w1, w2, gate, offs, out):
         quantize_slots(2)
         weight("w1", 0)
         weight("w1", 1)
-        hidden_slots(0)
-        hidden_slots(1)
         weight("w2", 0)
         weight("w2", 1)
+        hidden_slots(0)
+        hidden_slots(1)
         results_of(0)
         results_of(1)
         nc.sync.dma_start(out=gates[:], in_=gate[0:P, :])
+        shared_tokens(0)
+        shared_tokens(1)
+        shared_tokens(2)
         weight("w1", 2)
         weight("w1", 3)
         weight("w1", E)
@@ -210,9 +221,6 @@ def tile_moe_shr_mlp_silu_kernel(tc, xT, w1, w2, gate, offs, out):
         hidden_slots(3)
         results_of(2)
         results_of(3)
-        shared_tokens(0)
-        shared_tokens(1)
-        shared_tokens(2)
         for q in range(4):
             scatter(0, q)
         weight("w1", 4)
@@ -223,9 +231,9 @@ def tile_moe_shr_mlp_silu_kernel(tc, xT, w1, w2, gate, offs, out):
         hidden_slots(5)
         results_of(4)
         results_of(5)
-        shared_hidden(0)
         for q in range(4):
             scatter(1, q)
+        shared_hidden(0)
         weight("w2", E)
         shared_hidden(1)
         shared_hidden(2)

from contextlib import ExitStack

import concourse.mybir as mybir

K, T, E, C, H, N = 512, 1536, 6, 128, 512, 512
FLOPS = 2 * (E * C + T) * (K * H + H * N)
BYTES = 4 * (K * T + (E + 1) * (K * H + H * N) + E * C + N * T) + 2 * 128 * (E * C // 16)

P = 128
PACK = 4
PAIR = 2 * C
GROUP = 512
HALF = T // 2
VECTOR_COLUMNS = {("w1", 0): 192,("w1", 1): 0,("w2", 0): 0,("w2", 1): 256,("w1", 2): 192,("w1", 3): 0,("w2", 2): 0,("w2", 3): 256,("w1", 4): 192,("w1", 5): 0,("w2", 4): 0,("w2", 5): 256,("w1", 6): 0,("w2", 6): 512}

F32 = mybir.dt.float32
BF16 = mybir.dt.bfloat16
U32 = mybir.dt.uint32
I32 = mybir.dt.int32
U16 = mybir.dt.uint16
U8 = mybir.dt.uint8
FP8X4 = mybir.dt.float8_e4m3fn_x4
MULT = mybir.AluOpType.mult
ADD = mybir.AluOpType.add
SILU = mybir.ActivationFunctionType.Silu


def tile_moe_shr_mlp_silu_kernel(tc, xT, w1, w2, gate, offs, out):
    nc = tc.nc
    with ExitStack() as ctx:
        index = ctx.enter_context(tc.tile_pool(name="index", bufs=1))
        keep = ctx.enter_context(tc.tile_pool(name="keep", bufs=1))
        stage = ctx.enter_context(tc.tile_pool(name="stage", bufs=1))
        psum = ctx.enter_context(tc.psum_pool(name="psum", bufs=1))

        offsets = index.tile([P, E * C // 16], U16, name="offsets")
        xp = keep.tile([P, 2 * T * 2], BF16, name="xp", align_bytes=64)
        xg = keep.tile([P, E * C * PACK], BF16, name="xg", align_bytes=64)
        xs_codes = keep.tile([P, T], U32, name="xs_codes", align_bytes=64)
        xs_scales = keep.tile([P, T], U8, name="xs_scales", align_bytes=64)
        slot_codes = keep.tile([P, E * C], U32, name="slot_codes", align_bytes=64)
        slot_scales = keep.tile([P, E * C], U8, name="slot_scales", align_bytes=64)
        h_codes = keep.tile([P, E * C], U32, name="h_codes", align_bytes=64)
        h_scales = keep.tile([P, E * C], U8, name="h_scales", align_bytes=64)
        hs_codes = keep.tile([P, T], U32, name="hs_codes", align_bytes=64)
        hs_scales = keep.tile([P, T], U8, name="hs_scales", align_bytes=64)
        gates = keep.tile([P, E * C], F32, name="gates")
        acc = [keep.tile([P, T], F32, name=f"acc{q}") for q in range(4)]
        warm = keep.tile([P, 1], F32, name="warm")

        def quantize(rounded, codes, scales):
            nc.vector.quantize_mx(out=codes.bitcast(FP8X4), scales=scales, in_=rounded)

        w_codes = {}
        raws = {}

        def weight(layer, e):
            matrix = (w1 if layer == "w1" else w2)[e]
            raw = stage.tile([P, PACK, 512], F32, name="raw", bufs=8, align_bytes=64)
            nc.sync.dma_start(out=raw[:], in_=matrix.rearrange("(p j) w -> p j w", j=PACK))
            rounded = stage.tile([P, 512 * PACK], BF16, name="rounded", bufs=4, align_bytes=64)
            if layer == "w1":
                dst = rounded[:].rearrange("p (t m j) -> p m j t", t=PACK, j=PACK)
                src = raw[:].rearrange("p j (m t) -> p m j t", t=PACK)
            else:
                dst = rounded[:].rearrange("p (c i j) -> p c j i", i=4, j=PACK)
                src = raw[:].rearrange("p j (c i) -> p c j i", i=4)
            cut = 128 - VECTOR_COLUMNS.get((layer, e), 0) // 4
            if cut > 0:
                nc.scalar.copy(dst[:, :cut], src[:, :cut])
            if cut < 128 and layer == "w1":
                nc.vector.tensor_copy(dst[:, cut:], src[:, cut:])
            elif cut < 128:
                nc.vector.tensor_copy(
                    rounded[:, 16 * cut :].rearrange("p (c j) -> p c j", j=PACK),
                    raw[:, :, 4 * cut :].rearrange("p j c -> p c j"),
                )
            codes = keep.tile([P, 512], U32, name=f"codes_{layer}_{e}", align_bytes=64)
            scales = keep.tile([P, 512], U8, name=f"scales_{layer}_{e}", align_bytes=64)
            quantize(rounded[:], codes[:], scales[:])
            w_codes[layer, e] = (codes, scales)
            raws[layer, e] = raw

        def multiply(bank, w, w_cols, act_codes, act_scales):
            nc.tensor.matmul_mx(
                out=bank,
                lhsT=w[0][:, w_cols].bitcast(FP8X4),
                lhsT_scale=w[1][:, w_cols],
                rhs=act_codes.bitcast(FP8X4),
                rhs_scale=act_scales,
                start=True,
                stop=True,
            )

        def first_layer(e, act_codes, act_scales, hidden):
            bank = psum.tile([P, PACK, C], F32, name="bank_a", bufs=3)
            for t in range(PACK):
                multiply(bank[:, t, :], w_codes["w1", e], slice(128 * t, 128 * t + 128), act_codes, act_scales)
            nc.scalar.activation(
                hidden.rearrange("p (n t) -> p n t", t=PACK), bank[:].rearrange("p t n -> p n t"), SILU
            )

        nc.vector.memset(warm[:], 0.0)
        nc.scalar.activation(warm[:], warm[:], SILU)
        nc.vector.memset(acc[0][:], 0.0)
        nc.vector.memset(acc[1][:], 0.0)
        nc.gpsimd.memset(acc[2][:], 0.0)
        nc.gpsimd.memset(acc[3][:], 0.0)

        xp_words = xp[:].bitcast(I32).rearrange("p (u t) -> p u t", u=2)
        xp_pairs = xp[:].rearrange("p (u t e) -> p u t e", u=2, e=2)
        window = xp[:].bitcast(U32)
        slot_words = xg[:].bitcast(U32).rearrange("p (s u) -> p s u", u=2)
        x_rows = xT.rearrange("(p u e) t -> p u e t", u=2, e=2)

        def tokens(u, half, vector):
            cols = slice(half * HALF, (half + 1) * HALF)
            raw = stage.tile([P, 2, HALF], F32, name="raw", bufs=8, align_bytes=64)
            nc.sync.dma_start(out=raw[:], in_=x_rows[:, u, :, cols])
            if vector:
                nc.vector.tensor_copy(xp_pairs[:, u, cols, :], raw[:].rearrange("p e t -> p t e"))
            else:
                nc.scalar.copy(
                    xp_pairs[:, u, cols, :].rearrange("p (c i) e -> p c e i", i=4),
                    raw[:].rearrange("p e (c i) -> p c e i", i=4),
                )

        def gather(u):
            nc.vector.tensor_copy(slot_words[:, :, u], window[:, u * T : (u + 1) * T].indirect(offsets[:]))

        def quantize_slots(pair):
            slots = slice(pair * PAIR, (pair + 1) * PAIR)
            quantize(xg[:, pair * PAIR * PACK : (pair + 1) * PAIR * PACK], slot_codes[:, slots], slot_scales[:, slots])

        def shared_tokens(g):
            cols = slice(g * GROUP, (g + 1) * GROUP)
            xi = stage.tile([P, GROUP * PACK], BF16, name="xi", bufs=2, align_bytes=64)
            nc.vector.tensor_copy(
                xi[:].bitcast(I32).rearrange("p (t u) -> p t u", u=2),
                xp_words[:, :, cols].rearrange("p u t -> p t u"),
            )
            quantize(xi[:], xs_codes[:, cols], xs_scales[:, cols])

        def hidden_slots(e):
            slots = slice(e * C, (e + 1) * C)
            if e // 2 in (0, 1,):
                hidden = raws["w2", e][:].rearrange("p j w -> p (j w)").bitcast(BF16)[:, : C * PACK]
            else:
                fresh = stage.tile([P, C * PACK], BF16, name="hidden", bufs=3, align_bytes=64)
                hidden = fresh[:]
            first_layer(e, slot_codes[:, slots], slot_scales[:, slots], hidden)
            quantize(hidden, h_codes[:, slots], h_scales[:, slots])

        results = {}

        def results_of(e):
            pair, half = e // 2, e % 2
            if half == 0:
                results[pair] = stage.tile([P, 4, PAIR], F32, name="results", bufs=2)
            slots = slice(e * C, (e + 1) * C)
            bank = psum.tile([P, 4, C], F32, name="bank_y", bufs=2)
            for q in range(4):
                multiply(bank[:, q, :], w_codes["w2", e], slice(128 * q, 128 * q + 128), h_codes[:, slots], h_scales[:, slots])
            nc.scalar.copy(results[pair][:, :, half * C : (half + 1) * C], bank[:])

        def scatter(pair, q):
            listed = offsets[:, pair * PAIR // 16 : (pair + 1) * PAIR // 16]
            weights = gates[:, pair * PAIR : (pair + 1) * PAIR]
            nc.vector.tensor_tensor(acc[q][:].indirect(listed), results[pair][:, q, :], weights, MULT)

        def shared_hidden(g):
            hs = stage.tile([P, GROUP * PACK], BF16, name="hs", bufs=2, align_bytes=64)
            for b in range(GROUP // C):
                cols = slice(g * GROUP + b * C, g * GROUP + (b + 1) * C)
                first_layer(E, xs_codes[:, cols], xs_scales[:, cols], hs[:, b * 512 : (b + 1) * 512])
            cols = slice(g * GROUP, (g + 1) * GROUP)
            quantize(hs[:], hs_codes[:, cols], hs_scales[:, cols])

        def finish(q, g):
            cols = slice(g * GROUP, (g + 1) * GROUP)
            rows = slice(128 * q, 128 * q + 128)
            bank = psum.tile([P, GROUP], F32, name="bank_s", bufs=3)
            multiply(bank[:], w_codes["w2", E], rows, hs_codes[:, cols], hs_scales[:, cols])
            if q == 3:
                ys = stage.tile([P, GROUP], F32, name="ys", bufs=3)
                nc.scalar.copy(ys[:], bank[:])
                nc.gpsimd.tensor_tensor(acc[q][:, cols], ys[:], acc[q][:, cols], ADD)
            else:
                nc.vector.tensor_tensor(acc[q][:, cols], bank[:], acc[q][:, cols], ADD)
            queue = nc.scalar if q == 3 else nc.sync
            queue.dma_start(out=out[rows, cols], in_=acc[q][:, cols])

        tokens(0, 0, True)
        nc.sync.dma_start(offsets[:], offs)
        tokens(0, 1, True)
        tokens(1, 0, False)
        tokens(1, 1, False)
        gather(0)
        gather(1)
        quantize_slots(0)
        quantize_slots(1)
        quantize_slots(2)
        weight("w1", 0)
        weight("w1", 1)
        weight("w2", 0)
        weight("w2", 1)
        hidden_slots(0)
        hidden_slots(1)
        results_of(0)
        results_of(1)
        nc.sync.dma_start(out=gates[:], in_=gate[0:P, :])
        shared_tokens(0)
        shared_tokens(1)
        shared_tokens(2)
        weight("w1", 2)
        weight("w1", 3)
        weight("w1", E)
        weight("w2", 2)
        weight("w2", 3)
        hidden_slots(2)
        hidden_slots(3)
        results_of(2)
        results_of(3)
        for q in range(4):
            scatter(0, q)
        weight("w1", 4)
        weight("w1", 5)
        weight("w2", 4)
        weight("w2", 5)
        hidden_slots(4)
        hidden_slots(5)
        results_of(4)
        results_of(5)
        for q in range(4):
            scatter(1, q)
        shared_hidden(0)
        weight("w2", E)
        shared_hidden(1)
        shared_hidden(2)
        for q in range(4):
            scatter(2, q)
        for q in (3, 0, 1, 2):
            for g in range(T // GROUP):
                finish(q, g)
